import numpy as np
import ml_dtypes


def mxq(x, axis, fmt="e4m3"):
    dtype, down = {"e4m3": (ml_dtypes.float8_e4m3fn, 7), "e5m2": (ml_dtypes.float8_e5m2, 14)}[fmt]
    v = np.moveaxis(np.asarray(x, np.float32).astype(ml_dtypes.bfloat16).astype(np.float64), axis, -1)
    blocks = v.reshape(v.shape[:-1] + (-1, 32))
    amax = np.abs(blocks).max(-1, keepdims=True)
    byte = np.maximum(np.where(amax > 0, np.frexp(amax)[1] - 1 + 127, 0) - down, 1)
    scale = np.exp2(byte - 127.0)
    codes = (blocks / scale).astype(np.float32).astype(dtype).astype(np.float64)
    return np.moveaxis((codes * scale).reshape(v.shape), -1, axis)


WIDE = False


def mx_kscale(k):
    if not WIDE:
        return np.ones(k)
    levels = np.array([30, -30])
    if k % 512:
        return np.exp2(np.random.permutation(np.resize(levels, k // 32))).repeat(32)
    a = np.empty((k // 512, 16))
    for p in range(k // 512):
        a[p, :8] = np.random.permutation(np.resize(levels, 8))
        for g in range(8):
            far = levels[np.abs(levels - a[p, g]) >= 10]
            a[p, g + 8] = far[np.random.randint(len(far))]
    return np.exp2(a.ravel()).repeat(32)


def f64(x):
    return np.asarray(x).astype(np.float64)


def striped(idx):
    return np.tile(np.asarray(idx).reshape(-1, 16).T, (8, 1)).astype(np.uint16)


def unstriped(offs):
    return offs[:16].T.reshape(-1).astype(np.int64)


E2M1 = np.array([0.0, 0.5, 1.0, 1.5, 2.0, 3.0, 4.0, 6.0, -0.0, -0.5, -1.0, -1.5, -2.0, -3.0, -4.0, -6.0])


def pack_weight(w, fmt):
    k, n = w.shape
    w = f64(np.asarray(w, np.float32).astype(ml_dtypes.bfloat16)).reshape(k // 32, 32, n)
    amax = np.abs(w).max(1)
    if fmt in ("e4m3", "e5m2"):
        byte = np.frexp(amax)[1] - 1 + 127 - (7 if fmt == "e4m3" else 14)
    else:
        mant, ex = np.frexp(amax / 6.0)
        byte = np.where(mant > 0.5, ex, ex - 1) + 127
    byte = np.clip(np.where(amax > 0, byte, 1), 1, 254)
    scaled = (w * np.exp2(127.0 - byte)[:, None, :]).reshape(k, n).astype(np.float32)
    by_word = np.ascontiguousarray(scaled.reshape(k // 512, 128, 4, n).transpose(0, 1, 3, 2))
    if fmt in ("e4m3", "e5m2"):
        words = by_word.astype(ml_dtypes.float8_e4m3fn if fmt == "e4m3" else ml_dtypes.float8_e5m2).view(np.uint8)
    else:
        c = by_word.astype(ml_dtypes.float4_e2m1fn).view(np.uint8) & 0xF
        words = (c[..., 0::2] | (c[..., 1::2] << 4)).reshape(k // 512, 128, 2 * n)
    return np.ascontiguousarray(words), np.ascontiguousarray(byte.astype(np.uint8).reshape(k // 512, 16, n))


def unpack_weight(words, scales, fmt):
    g, _, n = scales.shape
    words = np.ascontiguousarray(words).reshape(g, 128, n, -1)
    if fmt in ("e4m3", "e5m2"):
        vals = words.view(ml_dtypes.float8_e4m3fn if fmt == "e4m3" else ml_dtypes.float8_e5m2).astype(np.float64)
    else:
        nib = np.empty((g, 128, n, 4), np.uint8)
        nib[..., 0::2] = words & 0xF
        nib[..., 1::2] = words >> 4
        vals = E2M1[nib]
    vals = vals * np.repeat(np.exp2(scales.astype(np.float64) - 127.0), 8, axis=1)[..., None]
    return vals.transpose(0, 1, 3, 2).reshape(g * 512, n)


K, T, J, R, C, O, N = 1024, 1024, 256, 512, 1024, 256, 256


def setup_inputs():
    n = np.random.standard_normal
    idx = np.random.permutation(T)[:J]
    idx2 = np.random.permutation(T)[:J]
    idx3 = np.random.permutation(C)[:J]
    idx4 = np.random.permutation(C)[:O]
    fk = mx_kscale(K)
    fr = mx_kscale(R)
    wp = pack_weight(n((K, R)) * 1 / np.sqrt(K) * fk[:, None] * fr, "e2m1")
    wbp = pack_weight(n((R, N)) * 1 / np.sqrt(R) / fr[:, None], "e5m2")
    return {
        "xf": (n((K, T))).astype(np.float32),
        "fk": (np.random.uniform(0.5, 2.0, (K, 1)) / fk[:, None]).astype(np.float32),
        "w_words": wp[0],
        "w_scales": wp[1],
        "oldh": (n((R, C)) * 0.7 * fr[:, None]).astype(np.float32),
        "wb_words": wbp[0],
        "wb_scales": wbp[1],
        "rs": (n((N, O))).astype(np.float32),
        "gm": (np.random.uniform(0.5, 2.0, (N, 1))).astype(np.float32),
        "offs": striped(idx),
        "offs2": striped(idx2),
        "offs3": striped(idx3),
        "offs4": striped(idx4),
    }


def reference(xf, fk, w_words, w_scales, oldh, wb_words, wb_scales, rs, gm, offs, offs2, offs3, offs4):
    idx = unstriped(offs)
    idx2 = unstriped(offs2)
    idx3 = unstriped(offs3)
    idx4 = unstriped(offs4)
    wu = unpack_weight(w_words, w_scales, "e2m1")
    wbu = unpack_weight(wb_words, wb_scales, "e5m2")
    u = np.maximum(f64(xf)[:, idx], f64(xf)[:, idx2]) * f64(fk)
    uq = mxq(u, 0, "e4m3")
    a = wu.T @ uq
    ha = np.maximum(a, 0.0)
    pw0 = np.zeros((R, C))
    pw0[:, idx3] = ha
    pg = pw0 + f64(oldh)
    hid = pg[:, idx4]
    hidq = mxq(hid, 0, "e5m2")
    p = wbu.T @ hidq
    y = f64(gm) * p + f64(rs)
    return y

@@ -1,0 +1,198 @@
+from contextlib import ExitStack
+
+import concourse.mybir as mybir
+
+K, T, J, R, C, O, N = 1024, 1024, 256, 512, 1024, 256, 256
+FLOPS = 2 * K * R * J + 2 * R * N * O
+
+F32 = mybir.dt.float32
+BF16 = mybir.dt.bfloat16
+I32 = mybir.dt.int32
+U32 = mybir.dt.uint32
+U16 = mybir.dt.uint16
+U8 = mybir.dt.uint8
+E4M3 = mybir.dt.float8_e4m3fn_x4
+E5M2 = mybir.dt.float8_e5m2_x4
+E2M1 = mybir.dt.float4_e2m1fn_x4
+ALU = mybir.AluOpType
+ACT = mybir.ActivationFunctionType
+
+P = 128
+PACK = 4
+PASSES = K // (P * PACK)
+LIST_COLS = 16
+HALF_COLS = LIST_COLS // 2
+
+
+def tile_list_page_largerpicks_residual_kernel(
+    tc, xf, fk, w_words, w_scales, oldh, wb_words, wb_scales, rs, gm, offs, offs2, offs3, offs4, out
+):
+    nc = tc.nc
+    with ExitStack() as ctx:
+        keep = ctx.enter_context(tc.tile_pool(name="keep", bufs=1))
+        psum = ctx.enter_context(tc.psum_pool(name="psum", bufs=1))
+
+        list1 = keep.tile([P, LIST_COLS], U16, name="list1")
+        list2 = keep.tile([P, LIST_COLS], U16, name="list2")
+        list3 = keep.tile([P, LIST_COLS], U16, name="list3")
+        list4 = keep.tile([P, LIST_COLS], U16, name="list4")
+
+        w_raw = keep.tile([P, PASSES * 2 * R], U8, name="w_raw", align_bytes=64)
+        w_codes = keep.tile([P, PASSES * 2 * R], U8, name="w_codes", align_bytes=64)
+        w_raw_plane = keep.tile([P, PASSES * R], U8, name="w_raw_plane", align_bytes=64)
+        w_plane = keep.tile([P, PASSES * R], U8, name="w_plane", align_bytes=64)
+        wb_codes = keep.tile([P, N], U32, name="wb_codes", align_bytes=64)
+        wb_plane = keep.tile([P, N], U8, name="wb_plane", align_bytes=64)
+        factor_k = keep.tile([P, PASSES, PACK], F32, name="factor_k")
+        factor_n = keep.tile([P, N // P], F32, name="factor_n")
+        residual = keep.tile([P, N // P, O], F32, name="residual")
+        tokens = [keep.tile([P, T], F32, name="tokens%d" % s) for s in range(PASSES * PACK)]
+        old = [keep.tile([P, C], F32, name="old%d" % t) for t in range(PACK)]
+        placed = [keep.tile([P, C], F32, name="placed%d" % t) for t in range(PACK)]
+        page = [keep.tile([P, C], F32, name="page%d" % t) for t in range(PACK)]
+
+        nc.vector.memset(w_raw_plane[:].bitcast(I32), 0)
+        nc.vector.memset(wb_plane[:].bitcast(I32), 0)
+
+        xf_rows = xf.rearrange("(a p i) t -> a i p t", a=PASSES, i=PACK)
+
+        def load_tokens(s):
+            nc.sync.dma_start(tokens[s][:], xf_rows[s // PACK, s % PACK])
+
+        def load_w_scales(q):
+            nc.sync.dma_start(
+                w_raw_plane[32 * q : 32 * q + 4, :].bitcast(I32).rearrange("p (a c) -> p a c", a=PASSES),
+                w_scales[:, 4 * q : 4 * q + 4, :].bitcast(I32).rearrange("a p c -> p a c"),
+            )
+
+        nc.sync.dma_start(list1[:], offs)
+        nc.sync.dma_start(list2[:], offs2)
+        nc.sync.dma_start(
+            w_raw[:].bitcast(I32).rearrange("p (a c) -> p a c", a=PASSES),
+            w_words.bitcast(I32).rearrange("a p c -> p a c"),
+        )
+        load_tokens(0)
+        nc.sync.dma_start(factor_k[:], fk.rearrange("(a p i) o -> p a (i o)", a=PASSES, i=PACK))
+        for s in range(1, PACK):
+            load_tokens(s)
+        for q in range(4):
+            load_w_scales(q)
+            load_tokens(PACK + q)
+        nc.sync.dma_start(list3[:], offs3)
+        old_rows = oldh.rearrange("(p t) c -> t p c", t=PACK)
+        for t in range(PACK):
+            nc.sync.dma_start(old[t][:], old_rows[t])
+        nc.sync.dma_start(list4[:], offs4)
+        nc.sync.dma_start(wb_codes[:].bitcast(I32), wb_words[0].rearrange("p n t -> p (n t)").bitcast(I32))
+        for q in range(4):
+            nc.sync.dma_start(
+                wb_plane[32 * q : 32 * q + 4, :].bitcast(I32), wb_scales[0, 4 * q : 4 * q + 4, :].bitcast(I32)
+            )
+        nc.sync.dma_start(residual[:], rs.rearrange("(h p) o -> p h o", p=P))
+        with nc.allow_non_contiguous_dma(reason="one factor a partition and half of n"):
+            nc.sync.dma_start(factor_n[:], gm.rearrange("(h p) o -> p (h o)", p=P))
+
+        for t in range(PACK):
+            nc.vector.memset(placed[t][:], 0.0)
+
+        nc.vector.tensor_copy(
+            w_codes[:].bitcast(U16).rearrange("p (a t m) -> p a t m", a=PASSES, t=PACK),
+            w_raw[:].bitcast(U16).rearrange("p (a m t) -> p a t m", a=PASSES, t=PACK),
+        )
+        nc.vector.tensor_copy(
+            w_plane[:].rearrange("p (a t m) -> p a t m", a=PASSES, t=PACK),
+            w_raw_plane[:].rearrange("p (a m t) -> p a t m", a=PASSES, t=PACK),
+        )
+
+        acc = [psum.tile([P, J], F32, name="acc%d" % t) for t in range(PACK)]
+        for a in range(PASSES):
+            u_bf = keep.tile([P, J, PACK], BF16, name="u_bf%d" % a, align_bytes=64)
+            for i in range(PACK):
+                s = PACK * a + i
+                first = keep.tile([P, J], F32, name="first%d" % s)
+                second = keep.tile([P, J], F32, name="second%d" % s)
+                larger = keep.tile([P, J], F32, name="larger%d" % s)
+                nc.scalar.activation(first[:], tokens[s][:].indirect(list1[:]), ACT.Copy)
+                if s % 2 == 1:
+                    nc.vector.tensor_copy(second[:, : J // 2], tokens[s][:].indirect(list2[:, :HALF_COLS]))
+                    nc.scalar.activation(second[:, J // 2 :], tokens[s][:].indirect(list2[:, HALF_COLS:]), ACT.Copy)
+                else:
+                    nc.scalar.activation(second[:], tokens[s][:].indirect(list2[:]), ACT.Copy)
+                halves = (slice(0, J // 2), slice(J // 2, J))
+                for cols in halves:
+                    nc.vector.tensor_tensor(larger[:, cols], first[:, cols], second[:, cols], ALU.max)
+                for cols in halves:
+                    nc.vector.tensor_scalar(u_bf[:, cols, i], larger[:, cols], factor_k[:, a, i : i + 1], None, ALU.mult)
+            u_codes = keep.tile([P, J], U32, name="u_codes%d" % a, align_bytes=64)
+            u_plane = keep.tile([P, J], U8, name="u_plane%d" % a, align_bytes=64)
+            nc.vector.quantize_mx(u_codes[:].bitcast(E4M3), u_plane[:], u_bf[:].rearrange("p j i -> p (j i)"))
+            for t in range(PACK):
+                col = a * R + t * P
+                nc.tensor.matmul_mx(
+                    acc[t][:],
+                    lhsT=w_codes[:, 2 * col : 2 * (col + P)].bitcast(E2M1),
+                    lhsT_scale=w_plane[:, col : col + P],
+                    rhs=u_codes[:].bitcast(E4M3),
+                    rhs_scale=u_plane[:],
+                    start=(a == 0),
+                    stop=(a == PASSES - 1),
+                )
+
+        ha = [keep.tile([P, J], F32, name="ha%d" % t) for t in range(PACK)]
+        hid = keep.tile([P, PACK, O], BF16, name="hid", align_bytes=64)
+
+        def relu_on_vector(t):
+            nc.vector.tensor_scalar(ha[t][:], acc[t][:], 0.0, None, ALU.max)
+
+        def relu_on_scalar(t):
+            nc.scalar.activation(ha[t][:], acc[t][:], ACT.Relu)
+
+        def place_on_scalar(t):
+            nc.scalar.activation(placed[t][:].indirect(list3[:]), ha[t][:], ACT.Copy)
+
+        def add_old(t):
+            nc.vector.tensor_tensor(page[t][:], placed[t][:], old[t][:], ALU.add)
+
+        def read_on_scalar(t):
+            nc.scalar.activation(hid[:, t, :], page[t][:].indirect(list4[:]), ACT.Copy)
+
+        relu_on_vector(0)
+        relu_on_scalar(1)
+        nc.vector.tensor_copy(placed[0][:].indirect(list3[:]), ha[0][:])
+        place_on_scalar(1)
+        relu_on_vector(2)
+        place_on_scalar(2)
+        add_old(0)
+        relu_on_scalar(3)
+        place_on_scalar(3)
+        add_old(1)
+        add_old(2)
+        add_old(3)
+        read_on_scalar(0)
+        read_on_scalar(1)
+        read_on_scalar(2)
+        nc.vector.tensor_copy(hid[:, 3, :], page[3][:].indirect(list4[:]))
+
+        hid_bf = keep.tile([P, O, PACK], BF16, name="hid_bf", align_bytes=64)
+        nc.vector.tensor_copy(hid_bf[:], hid[:].rearrange("p t o -> p o t"))
+        hid_codes = keep.tile([P, O], U32, name="hid_codes", align_bytes=64)
+        hid_plane = keep.tile([P, O], U8, name="hid_plane", align_bytes=64)
+        nc.vector.quantize_mx(hid_codes[:].bitcast(E5M2), hid_plane[:], hid_bf[:].rearrange("p o t -> p (o t)"))
+
+        for h in range(N // P):
+            prod = psum.tile([P, O], F32, name="prod%d" % h)
+            nc.tensor.matmul_mx(
+                prod[:],
+                lhsT=wb_codes[:, h * P : (h + 1) * P].bitcast(E5M2),
+                lhsT_scale=wb_plane[:, h * P : (h + 1) * P],
+                rhs=hid_codes[:].bitcast(E5M2),
+                rhs_scale=hid_plane[:],
+                start=True,
+                stop=True,
+            )
+            result = keep.tile([P, O], F32, name="result%d" % h)
+            nc.vector.scalar_tensor_tensor(
+                result[:], prod[:], factor_n[:, h : h + 1], residual[:, h, :], ALU.mult, ALU.add
+            )
+            queue = nc.sync if h == 0 else nc.scalar
+            queue.dma_start(out[h * P : (h + 1) * P, :], result[:])

@@ -22,6 +22,7 @@ PACK = 4
 PASSES = K // (P * PACK)
 LIST_COLS = 16
 HALF_COLS = LIST_COLS // 2
+RUN = 4
 
 
 def tile_list_page_largerpicks_residual_kernel(
@@ -48,9 +49,14 @@ def tile_list_page_largerpicks_residual_kernel(
         residual = keep.tile([P, N // P, O], F32, name="residual")
         tokens = [keep.tile([P, T], F32, name="tokens%d" % s) for s in range(PASSES * PACK)]
         old = [keep.tile([P, C], F32, name="old%d" % t) for t in range(PACK)]
-        placed = [keep.tile([P, C], F32, name="placed%d" % t) for t in range(PACK)]
+        cleared = [keep.tile([P, C], F32, name="placed%d" % t) for t in range(PACK - 1)]
+        placed = cleared + cleared[:1]
         page = [keep.tile([P, C], F32, name="page%d" % t) for t in range(PACK)]
 
+        warm_in = keep.tile([P, 1], F32, name="warm_in")
+        warm_out = keep.tile([P, 1], F32, name="warm_out")
+        nc.gpsimd.memset(warm_in[:], 0.0)
+        nc.scalar.activation(warm_out[:], warm_in[:], ACT.Relu)
         nc.vector.memset(w_raw_plane[:].bitcast(I32), 0)
         nc.vector.memset(wb_plane[:].bitcast(I32), 0)
 
@@ -65,19 +71,22 @@ def tile_list_page_largerpicks_residual_kernel(
                 w_scales[:, 4 * q : 4 * q + 4, :].bitcast(I32).rearrange("a p c -> p a c"),
             )
 
+        load_tokens(0)
         nc.sync.dma_start(list1[:], offs)
         nc.sync.dma_start(list2[:], offs2)
         nc.sync.dma_start(
             w_raw[:].bitcast(I32).rearrange("p (a c) -> p a c", a=PASSES),
             w_words.bitcast(I32).rearrange("a p c -> p a c"),
         )
-        load_tokens(0)
-        nc.sync.dma_start(factor_k[:], fk.rearrange("(a p i) o -> p a (i o)", a=PASSES, i=PACK))
-        for s in range(1, PACK):
-            load_tokens(s)
-        for q in range(4):
+        for q in range(3):
             load_w_scales(q)
-            load_tokens(PACK + q)
+        load_tokens(1)
+        load_w_scales(3)
+        load_tokens(2)
+        load_tokens(3)
+        nc.sync.dma_start(factor_k[:], fk.rearrange("(a p i) o -> p a (i o)", a=PASSES, i=PACK))
+        for s in range(PACK, PASSES * PACK):
+            load_tokens(s)
         nc.sync.dma_start(list3[:], offs3)
         old_rows = oldh.rearrange("(p t) c -> t p c", t=PACK)
         for t in range(PACK):
@@ -92,8 +101,8 @@ def tile_list_page_largerpicks_residual_kernel(
         with nc.allow_non_contiguous_dma(reason="one factor a partition and half of n"):
             nc.sync.dma_start(factor_n[:], gm.rearrange("(h p) o -> p (h o)", p=P))
 
-        for t in range(PACK):
-            nc.vector.memset(placed[t][:], 0.0)
+        for tile in cleared:
+            nc.vector.memset(tile[:], 0.0)
 
         nc.vector.tensor_copy(
             w_codes[:].bitcast(U16).rearrange("p (a t m) -> p a t m", a=PASSES, t=PACK),
@@ -106,26 +115,39 @@ def tile_list_page_largerpicks_residual_kernel(
 
         acc = [psum.tile([P, J], F32, name="acc%d" % t) for t in range(PACK)]
         for a in range(PASSES):
-            u_bf = keep.tile([P, J, PACK], BF16, name="u_bf%d" % a, align_bytes=64)
-            for i in range(PACK):
-                s = PACK * a + i
-                first = keep.tile([P, J], F32, name="first%d" % s)
-                second = keep.tile([P, J], F32, name="second%d" % s)
-                larger = keep.tile([P, J], F32, name="larger%d" % s)
-                nc.scalar.activation(first[:], tokens[s][:].indirect(list1[:]), ACT.Copy)
-                if s % 2 == 1:
-                    nc.vector.tensor_copy(second[:, : J // 2], tokens[s][:].indirect(list2[:, :HALF_COLS]))
-                    nc.scalar.activation(second[:, J // 2 :], tokens[s][:].indirect(list2[:, HALF_COLS:]), ACT.Copy)
-                else:
-                    nc.scalar.activation(second[:], tokens[s][:].indirect(list2[:]), ACT.Copy)
-                halves = (slice(0, J // 2), slice(J // 2, J))
-                for cols in halves:
-                    nc.vector.tensor_tensor(larger[:, cols], first[:, cols], second[:, cols], ALU.max)
-                for cols in halves:
-                    nc.vector.tensor_scalar(u_bf[:, cols, i], larger[:, cols], factor_k[:, a, i : i + 1], None, ALU.mult)
+            first = keep.tile([P, PACK, J], F32, name="first%d" % a)
+            second = keep.tile([P, PACK, J], F32, name="second%d" % a)
+            larger = keep.tile([P, PACK, J], F32, name="larger%d" % a)
+            u_bf = keep.tile([P, J * PACK], BF16, name="u_bf%d" % a, align_bytes=64)
             u_codes = keep.tile([P, J], U32, name="u_codes%d" % a, align_bytes=64)
             u_plane = keep.tile([P, J], U8, name="u_plane%d" % a, align_bytes=64)
-            nc.vector.quantize_mx(u_codes[:].bitcast(E4M3), u_plane[:], u_bf[:].rearrange("p j i -> p (j i)"))
+            halves = (slice(0, J // 2), slice(J // 2, J))
+            for i in range(PACK):
+                window = tokens[PACK * a + i]
+                nc.scalar.activation(first[:, i, :], window[:].indirect(list1[:]), ACT.Copy)
+                if i == PACK - 1:
+                    nc.vector.tensor_copy(second[:, i, :], window[:].indirect(list2[:]))
+                else:
+                    nc.scalar.activation(second[:, i, :], window[:].indirect(list2[:]), ACT.Copy)
+                if i < PACK - 2:
+                    nc.vector.tensor_tensor(larger[:, i, :], first[:, i, :], second[:, i, :], ALU.max)
+            for cols in halves:
+                nc.vector.tensor_tensor(
+                    larger[:, PACK - 2 :, cols], first[:, PACK - 2 :, cols], second[:, PACK - 2 :, cols], ALU.max
+                )
+            for cols in halves:
+                nc.vector.tensor_tensor(
+                    u_bf[:, PACK * cols.start : PACK * cols.stop].rearrange("p (c e i) -> p c i e", e=RUN, i=PACK),
+                    larger[:, :, cols].rearrange("p i (c e) -> p c i e", e=RUN),
+                    factor_k[:, a, :]
+                    .rearrange("p (c i e) -> p c i e", c=1, e=1)
+                    .broadcast_to([P, J // 2 // RUN, PACK, RUN]),
+                    ALU.mult,
+                )
+            for cols in halves:
+                nc.vector.quantize_mx(
+                    u_codes[:, cols].bitcast(E4M3), u_plane[:, cols], u_bf[:, PACK * cols.start : PACK * cols.stop]
+                )
             for t in range(PACK):
                 col = a * R + t * P
                 nc.tensor.matmul_mx(
@@ -159,40 +181,51 @@ def tile_list_page_largerpicks_residual_kernel(
         relu_on_vector(0)
         relu_on_scalar(1)
         nc.vector.tensor_copy(placed[0][:].indirect(list3[:]), ha[0][:])
+        relu_on_scalar(2)
         place_on_scalar(1)
-        relu_on_vector(2)
-        place_on_scalar(2)
+        relu_on_vector(3)
         add_old(0)
-        relu_on_scalar(3)
-        place_on_scalar(3)
+        place_on_scalar(2)
         add_old(1)
+        place_on_scalar(3)
         add_old(2)
         add_old(3)
         read_on_scalar(0)
         read_on_scalar(1)
         read_on_scalar(2)
-        nc.vector.tensor_copy(hid[:, 3, :], page[3][:].indirect(list4[:]))
+        nc.vector.tensor_copy(hid[:, 3, : O // 2], page[3][:].indirect(list4[:, :HALF_COLS]))
+        nc.vector.tensor_copy(hid[:, 3, O // 2 :], page[3][:].indirect(list4[:, HALF_COLS:]))
 
-        hid_bf = keep.tile([P, O, PACK], BF16, name="hid_bf", align_bytes=64)
-        nc.vector.tensor_copy(hid_bf[:], hid[:].rearrange("p t o -> p o t"))
-        hid_codes = keep.tile([P, O], U32, name="hid_codes", align_bytes=64)
-        hid_plane = keep.tile([P, O], U8, name="hid_plane", align_bytes=64)
-        nc.vector.quantize_mx(hid_codes[:].bitcast(E5M2), hid_plane[:], hid_bf[:].rearrange("p o t -> p (o t)"))
-
-        for h in range(N // P):
-            prod = psum.tile([P, O], F32, name="prod%d" % h)
-            nc.tensor.matmul_mx(
-                prod[:],
-                lhsT=wb_codes[:, h * P : (h + 1) * P].bitcast(E5M2),
-                lhsT_scale=wb_plane[:, h * P : (h + 1) * P],
-                rhs=hid_codes[:].bitcast(E5M2),
-                rhs_scale=hid_plane[:],
-                start=True,
-                stop=True,
+        half = O // 2
+        hid_bf = [keep.tile([P, half, PACK], BF16, name="hid_bf%d" % g, align_bytes=64) for g in range(2)]
+        hid_codes = [keep.tile([P, half], U32, name="hid_codes%d" % g, align_bytes=64) for g in range(2)]
+        hid_plane = [keep.tile([P, half], U8, name="hid_plane%d" % g, align_bytes=64) for g in range(2)]
+        for g in range(2):
+            nc.vector.tensor_copy(
+                hid_bf[g][:].rearrange("p (c e) t -> p c t e", e=RUN),
+                hid[:, :, g * half : (g + 1) * half].rearrange("p t (c e) -> p c t e", e=RUN),
             )
-            result = keep.tile([P, O], F32, name="result%d" % h)
-            nc.vector.scalar_tensor_tensor(
-                result[:], prod[:], factor_n[:, h : h + 1], residual[:, h, :], ALU.mult, ALU.add
+        for g in range(2):
+            nc.vector.quantize_mx(
+                hid_codes[g][:].bitcast(E5M2), hid_plane[g][:], hid_bf[g][:].rearrange("p o t -> p (o t)")
             )
-            queue = nc.sync if h == 0 else nc.scalar
-            queue.dma_start(out[h * P : (h + 1) * P, :], result[:])
+        out_rows = out.rearrange("(h p) o -> p h o", p=P)
+        for g in range(2):
+            cols = slice(g * half, (g + 1) * half)
+            result = keep.tile([P, N // P, half], F32, name="result%d" % g)
+            for h in range(N // P):
+                prod = psum.tile([P, half], F32, name="prod%d_%d" % (g, h))
+                nc.tensor.matmul_mx(
+                    prod[:],
+                    lhsT=wb_codes[:, h * P : (h + 1) * P].bitcast(E5M2),
+                    lhsT_scale=wb_plane[:, h * P : (h + 1) * P],
+                    rhs=hid_codes[g][:].bitcast(E5M2),
+                    rhs_scale=hid_plane[g][:],
+                    start=True,
+                    stop=True,
+                )
+                nc.vector.scalar_tensor_tensor(
+                    result[:, h, :], prod[:], factor_n[:, h : h + 1], residual[:, h, cols], ALU.mult, ALU.add
+                )
+            queue = nc.scalar if g == 0 else nc.sync
+            queue.dma_start(out_rows[:, :, cols], result[:])

@@ -125,12 +125,12 @@ def tile_list_page_largerpicks_residual_kernel(
             for i in range(PACK):
                 window = tokens[PACK * a + i]
                 nc.scalar.activation(first[:, i, :], window[:].indirect(list1[:]), ACT.Copy)
-                if i == PACK - 1:
+                if i % 2 == 1:
                     nc.vector.tensor_copy(second[:, i, :], window[:].indirect(list2[:]))
                 else:
                     nc.scalar.activation(second[:, i, :], window[:].indirect(list2[:]), ACT.Copy)
-                if i < PACK - 2:
-                    nc.vector.tensor_tensor(larger[:, i, :], first[:, i, :], second[:, i, :], ALU.max)
+                if i == 1:
+                    nc.vector.tensor_tensor(larger[:, :2, :], first[:, :2, :], second[:, :2, :], ALU.max)
             for cols in halves:
                 nc.vector.tensor_tensor(
                     larger[:, PACK - 2 :, cols], first[:, PACK - 2 :, cols], second[:, PACK - 2 :, cols], ALU.max
@@ -148,17 +148,29 @@ def tile_list_page_largerpicks_residual_kernel(
                 nc.vector.quantize_mx(
                     u_codes[:, cols].bitcast(E4M3), u_plane[:, cols], u_bf[:, PACK * cols.start : PACK * cols.stop]
                 )
-            for t in range(PACK):
+
+            def multiply(t, cols, stop):
                 col = a * R + t * P
                 nc.tensor.matmul_mx(
-                    acc[t][:],
+                    acc[t][:, cols],
                     lhsT=w_codes[:, 2 * col : 2 * (col + P)].bitcast(E2M1),
                     lhsT_scale=w_plane[:, col : col + P],
-                    rhs=u_codes[:].bitcast(E4M3),
-                    rhs_scale=u_plane[:],
+                    rhs=u_codes[:, cols].bitcast(E4M3),
+                    rhs_scale=u_plane[:, cols],
                     start=(a == 0),
-                    stop=(a == PASSES - 1),
+                    stop=stop,
                 )
+
+            whole = slice(0, J)
+            if a < PASSES - 1:
+                for t in range(PACK):
+                    multiply(t, whole, False)
+            else:
+                for cols in halves:
+                    for t in range(2):
+                        multiply(t, cols, cols.stop == J)
+                for t in range(2, PACK):
+                    multiply(t, whole, True)
 
         ha = [keep.tile([P, J], F32, name="ha%d" % t) for t in range(PACK)]
         hid = keep.tile([P, PACK, O], BF16, name="hid", align_bytes=64)
@@ -180,8 +192,8 @@ def tile_list_page_largerpicks_residual_kernel(
 
         relu_on_vector(0)
         relu_on_scalar(1)
+        relu_on_vector(2)
         nc.vector.tensor_copy(placed[0][:].indirect(list3[:]), ha[0][:])
-        relu_on_scalar(2)
         place_on_scalar(1)
         relu_on_vector(3)
         add_old(0)
@@ -212,8 +224,8 @@ def tile_list_page_largerpicks_residual_kernel(
         out_rows = out.rearrange("(h p) o -> p h o", p=P)
         for g in range(2):
             cols = slice(g * half, (g + 1) * half)
-            result = keep.tile([P, N // P, half], F32, name="result%d" % g)
             for h in range(N // P):
+                result = keep.tile([P, half], F32, name="result%d_%d" % (g, h))
                 prod = psum.tile([P, half], F32, name="prod%d_%d" % (g, h))
                 nc.tensor.matmul_mx(
                     prod[:],
@@ -225,7 +237,7 @@ def tile_list_page_largerpicks_residual_kernel(
                     stop=True,
                 )
                 nc.vector.scalar_tensor_tensor(
-                    result[:, h, :], prod[:], factor_n[:, h : h + 1], residual[:, h, cols], ALU.mult, ALU.add
+                    result[:], prod[:], factor_n[:, h : h + 1], residual[:, h, cols], ALU.mult, ALU.add
                 )
-            queue = nc.scalar if g == 0 else nc.sync
-            queue.dma_start(out_rows[:, :, cols], result[:])
+                queue = nc.scalar if h == 0 else nc.sync
+                queue.dma_start(out_rows[:, h, cols], result[:])

from contextlib import ExitStack

import concourse.mybir as mybir

K, T, J, R, C, O, N = 1024, 1024, 256, 512, 1024, 256, 256
FLOPS = 2 * K * R * J + 2 * R * N * O

F32 = mybir.dt.float32
BF16 = mybir.dt.bfloat16
I32 = mybir.dt.int32
U32 = mybir.dt.uint32
U16 = mybir.dt.uint16
U8 = mybir.dt.uint8
E4M3 = mybir.dt.float8_e4m3fn_x4
E5M2 = mybir.dt.float8_e5m2_x4
E2M1 = mybir.dt.float4_e2m1fn_x4
ALU = mybir.AluOpType
ACT = mybir.ActivationFunctionType

P = 128
PACK = 4
PASSES = K // (P * PACK)
LIST_COLS = 16
HALF_COLS = LIST_COLS // 2
RUN = 4


def tile_list_page_largerpicks_residual_kernel(
    tc, xf, fk, w_words, w_scales, oldh, wb_words, wb_scales, rs, gm, offs, offs2, offs3, offs4, out
):
    nc = tc.nc
    with ExitStack() as ctx:
        keep = ctx.enter_context(tc.tile_pool(name="keep", bufs=1))
        psum = ctx.enter_context(tc.psum_pool(name="psum", bufs=1))

        list1 = keep.tile([P, LIST_COLS], U16, name="list1")
        list2 = keep.tile([P, LIST_COLS], U16, name="list2")
        list3 = keep.tile([P, LIST_COLS], U16, name="list3")
        list4 = keep.tile([P, LIST_COLS], U16, name="list4")

        w_raw = keep.tile([P, PASSES * 2 * R], U8, name="w_raw", align_bytes=64)
        w_codes = keep.tile([P, PASSES * 2 * R], U8, name="w_codes", align_bytes=64)
        w_raw_plane = keep.tile([P, PASSES * R], U8, name="w_raw_plane", align_bytes=64)
        w_plane = keep.tile([P, PASSES * R], U8, name="w_plane", align_bytes=64)
        wb_codes = keep.tile([P, N], U32, name="wb_codes", align_bytes=64)
        wb_plane = keep.tile([P, N], U8, name="wb_plane", align_bytes=64)
        factor_k = keep.tile([P, PASSES, PACK], F32, name="factor_k")
        factor_n = keep.tile([P, N // P], F32, name="factor_n")
        residual = keep.tile([P, N // P, O], F32, name="residual")
        tokens = [keep.tile([P, T], F32, name="tokens%d" % s) for s in range(PASSES * PACK)]
        old = [keep.tile([P, C], F32, name="old%d" % t) for t in range(PACK)]
        cleared = [keep.tile([P, C], F32, name="placed%d" % t) for t in range(PACK - 1)]
        placed = cleared + cleared[:1]
        page = [keep.tile([P, C], F32, name="page%d" % t) for t in range(PACK)]

        warm_in = keep.tile([P, 1], F32, name="warm_in")
        warm_out = keep.tile([P, 1], F32, name="warm_out")
        nc.gpsimd.memset(warm_in[:], 0.0)
        nc.scalar.activation(warm_out[:], warm_in[:], ACT.Relu)
        nc.vector.memset(w_raw_plane[:].bitcast(I32), 0)
        nc.vector.memset(wb_plane[:].bitcast(I32), 0)

        xf_rows = xf.rearrange("(a p i) t -> a i p t", a=PASSES, i=PACK)

        def load_tokens(s):
            nc.sync.dma_start(tokens[s][:], xf_rows[s // PACK, s % PACK])

        def load_w_scales(q):
            nc.sync.dma_start(
                w_raw_plane[32 * q : 32 * q + 4, :].bitcast(I32).rearrange("p (a c) -> p a c", a=PASSES),
                w_scales[:, 4 * q : 4 * q + 4, :].bitcast(I32).rearrange("a p c -> p a c"),
            )

        load_tokens(0)
        nc.sync.dma_start(list1[:], offs)
        nc.sync.dma_start(list2[:], offs2)
        nc.sync.dma_start(
            w_raw[:].bitcast(I32).rearrange("p (a c) -> p a c", a=PASSES),
            w_words.bitcast(I32).rearrange("a p c -> p a c"),
        )
        for q in range(3):
            load_w_scales(q)
        load_tokens(1)
        load_w_scales(3)
        load_tokens(2)
        load_tokens(3)
        nc.sync.dma_start(factor_k[:], fk.rearrange("(a p i) o -> p a (i o)", a=PASSES, i=PACK))
        for s in range(PACK, PASSES * PACK):
            load_tokens(s)
        nc.sync.dma_start(list3[:], offs3)
        old_rows = oldh.rearrange("(p t) c -> t p c", t=PACK)
        for t in range(PACK):
            nc.sync.dma_start(old[t][:], old_rows[t])
        nc.sync.dma_start(list4[:], offs4)
        nc.sync.dma_start(wb_codes[:].bitcast(I32), wb_words[0].rearrange("p n t -> p (n t)").bitcast(I32))
        for q in range(4):
            nc.sync.dma_start(
                wb_plane[32 * q : 32 * q + 4, :].bitcast(I32), wb_scales[0, 4 * q : 4 * q + 4, :].bitcast(I32)
            )
        nc.sync.dma_start(residual[:], rs.rearrange("(h p) o -> p h o", p=P))
        with nc.allow_non_contiguous_dma(reason="one factor a partition and half of n"):
            nc.sync.dma_start(factor_n[:], gm.rearrange("(h p) o -> p (h o)", p=P))

        for tile in cleared:
            nc.vector.memset(tile[:], 0.0)

        nc.vector.tensor_copy(
            w_codes[:].bitcast(U16).rearrange("p (a t m) -> p a t m", a=PASSES, t=PACK),
            w_raw[:].bitcast(U16).rearrange("p (a m t) -> p a t m", a=PASSES, t=PACK),
        )
        nc.vector.tensor_copy(
            w_plane[:].rearrange("p (a t m) -> p a t m", a=PASSES, t=PACK),
            w_raw_plane[:].rearrange("p (a m t) -> p a t m", a=PASSES, t=PACK),
        )

        acc = [psum.tile([P, J], F32, name="acc%d" % t) for t in range(PACK)]
        for a in range(PASSES):
            first = keep.tile([P, PACK, J], F32, name="first%d" % a)
            second = keep.tile([P, PACK, J], F32, name="second%d" % a)
            larger = keep.tile([P, PACK, J], F32, name="larger%d" % a)
            u_bf = keep.tile([P, J * PACK], BF16, name="u_bf%d" % a, align_bytes=64)
            u_codes = keep.tile([P, J], U32, name="u_codes%d" % a, align_bytes=64)
            u_plane = keep.tile([P, J], U8, name="u_plane%d" % a, align_bytes=64)
            halves = (slice(0, J // 2), slice(J // 2, J))
            for i in range(PACK):
                window = tokens[PACK * a + i]
                nc.scalar.activation(first[:, i, :], window[:].indirect(list1[:]), ACT.Copy)
                if i % 2 == 1:
                    nc.vector.tensor_copy(second[:, i, :], window[:].indirect(list2[:]))
                else:
                    nc.scalar.activation(second[:, i, :], window[:].indirect(list2[:]), ACT.Copy)
                if i == 1:
                    nc.vector.tensor_tensor(larger[:, :2, :], first[:, :2, :], second[:, :2, :], ALU.max)
            for cols in halves:
                nc.vector.tensor_tensor(
                    larger[:, PACK - 2 :, cols], first[:, PACK - 2 :, cols], second[:, PACK - 2 :, cols], ALU.max
                )
            for cols in halves:
                nc.vector.tensor_tensor(
                    u_bf[:, PACK * cols.start : PACK * cols.stop].rearrange("p (c e i) -> p c i e", e=RUN, i=PACK),
                    larger[:, :, cols].rearrange("p i (c e) -> p c i e", e=RUN),
                    factor_k[:, a, :]
                    .rearrange("p (c i e) -> p c i e", c=1, e=1)
                    .broadcast_to([P, J // 2 // RUN, PACK, RUN]),
                    ALU.mult,
                )
            for cols in halves:
                nc.vector.quantize_mx(
                    u_codes[:, cols].bitcast(E4M3), u_plane[:, cols], u_bf[:, PACK * cols.start : PACK * cols.stop]
                )

            def multiply(t, cols, stop):
                col = a * R + t * P
                nc.tensor.matmul_mx(
                    acc[t][:, cols],
                    lhsT=w_codes[:, 2 * col : 2 * (col + P)].bitcast(E2M1),
                    lhsT_scale=w_plane[:, col : col + P],
                    rhs=u_codes[:, cols].bitcast(E4M3),
                    rhs_scale=u_plane[:, cols],
                    start=(a == 0),
                    stop=stop,
                )

            whole = slice(0, J)
            if a < PASSES - 1:
                for t in range(PACK):
                    multiply(t, whole, False)
            else:
                for cols in halves:
                    for t in range(2):
                        multiply(t, cols, cols.stop == J)
                for t in range(2, PACK):
                    multiply(t, whole, True)

        ha = [keep.tile([P, J], F32, name="ha%d" % t) for t in range(PACK)]
        hid = keep.tile([P, PACK, O], BF16, name="hid", align_bytes=64)

        def relu_on_vector(t):
            nc.vector.tensor_scalar(ha[t][:], acc[t][:], 0.0, None, ALU.max)

        def relu_on_scalar(t):
            nc.scalar.activation(ha[t][:], acc[t][:], ACT.Relu)

        def place_on_scalar(t):
            nc.scalar.activation(placed[t][:].indirect(list3[:]), ha[t][:], ACT.Copy)

        def add_old(t):
            nc.vector.tensor_tensor(page[t][:], placed[t][:], old[t][:], ALU.add)

        def read_on_scalar(t):
            nc.scalar.activation(hid[:, t, :], page[t][:].indirect(list4[:]), ACT.Copy)

        relu_on_vector(0)
        relu_on_scalar(1)
        relu_on_vector(2)
        nc.vector.tensor_copy(placed[0][:].indirect(list3[:]), ha[0][:])
        place_on_scalar(1)
        relu_on_vector(3)
        add_old(0)
        place_on_scalar(2)
        add_old(1)
        place_on_scalar(3)
        add_old(2)
        add_old(3)
        read_on_scalar(0)
        read_on_scalar(1)
        read_on_scalar(2)
        nc.vector.tensor_copy(hid[:, 3, : O // 2], page[3][:].indirect(list4[:, :HALF_COLS]))
        nc.vector.tensor_copy(hid[:, 3, O // 2 :], page[3][:].indirect(list4[:, HALF_COLS:]))

        half = O // 2
        hid_bf = [keep.tile([P, half, PACK], BF16, name="hid_bf%d" % g, align_bytes=64) for g in range(2)]
        hid_codes = [keep.tile([P, half], U32, name="hid_codes%d" % g, align_bytes=64) for g in range(2)]
        hid_plane = [keep.tile([P, half], U8, name="hid_plane%d" % g, align_bytes=64) for g in range(2)]
        for g in range(2):
            nc.vector.tensor_copy(
                hid_bf[g][:].rearrange("p (c e) t -> p c t e", e=RUN),
                hid[:, :, g * half : (g + 1) * half].rearrange("p t (c e) -> p c t e", e=RUN),
            )
        for g in range(2):
            nc.vector.quantize_mx(
                hid_codes[g][:].bitcast(E5M2), hid_plane[g][:], hid_bf[g][:].rearrange("p o t -> p (o t)")
            )
        out_rows = out.rearrange("(h p) o -> p h o", p=P)
        for g in range(2):
            cols = slice(g * half, (g + 1) * half)
            for h in range(N // P):
                result = keep.tile([P, half], F32, name="result%d_%d" % (g, h))
                prod = psum.tile([P, half], F32, name="prod%d_%d" % (g, h))
                nc.tensor.matmul_mx(
                    prod[:],
                    lhsT=wb_codes[:, h * P : (h + 1) * P].bitcast(E5M2),
                    lhsT_scale=wb_plane[:, h * P : (h + 1) * P],
                    rhs=hid_codes[g][:].bitcast(E5M2),
                    rhs_scale=hid_plane[g][:],
                    start=True,
                    stop=True,
                )
                nc.vector.scalar_tensor_tensor(
                    result[:], prod[:], factor_n[:, h : h + 1], residual[:, h, cols], ALU.mult, ALU.add
                )
                queue = nc.scalar if h == 0 else nc.sync
                queue.dma_start(out_rows[:, h, cols], result[:])
